import numpy as np
import ml_dtypes


def mxq(x, axis, fmt="e4m3"):
    dtype, down = {"e4m3": (ml_dtypes.float8_e4m3fn, 7), "e5m2": (ml_dtypes.float8_e5m2, 14)}[fmt]
    v = np.moveaxis(np.asarray(x, np.float32).astype(ml_dtypes.bfloat16).astype(np.float64), axis, -1)
    blocks = v.reshape(v.shape[:-1] + (-1, 32))
    amax = np.abs(blocks).max(-1, keepdims=True)
    byte = np.maximum(np.where(amax > 0, np.frexp(amax)[1] - 1 + 127, 0) - down, 1)
    scale = np.exp2(byte - 127.0)
    codes = (blocks / scale).astype(np.float32).astype(dtype).astype(np.float64)
    return np.moveaxis((codes * scale).reshape(v.shape), -1, axis)


WIDE = False


def mx_kscale(k):
    if not WIDE:
        return np.ones(k)
    levels = np.array([24, -24, 12, -12, 0])
    if k % 512:
        return np.exp2(np.random.permutation(np.resize(levels, k // 32))).repeat(32)
    a = np.empty((k // 512, 16))
    for p in range(k // 512):
        a[p, :8] = np.random.permutation(np.resize(levels, 8))
        for g in range(8):
            far = levels[np.abs(levels - a[p, g]) >= 10]
            a[p, g + 8] = far[np.random.randint(len(far))]
    return np.exp2(a.ravel()).repeat(32)


def f64(x):
    return np.asarray(x).astype(np.float64)


def striped(idx):
    return np.tile(idx.reshape(-1, 16).T, (8, 1)).astype(np.uint16)


def unstriped(offs):
    return offs[:16].T.reshape(-1).astype(np.int64)


def striped8(idx):
    return np.concatenate([v.reshape(-1, 16).T for v in idx]).astype(np.uint16)


def unstriped8(offs):
    return np.stack([offs[16 * g:16 * g + 16].T.reshape(-1) for g in range(8)]).astype(np.int64)


E2M1 = np.array([0.0, 0.5, 1.0, 1.5, 2.0, 3.0, 4.0, 6.0, -0.0, -0.5, -1.0, -1.5, -2.0, -3.0, -4.0, -6.0])


def pack_weight(w, fmt):
    k, n = w.shape
    w = f64(np.asarray(w, np.float32).astype(ml_dtypes.bfloat16)).reshape(k // 32, 32, n)
    amax = np.abs(w).max(1)
    if fmt == "e4m3":
        byte = np.frexp(amax)[1] - 1 + 127 - 7
    else:
        mant, ex = np.frexp(amax / 6.0)
        byte = np.where(mant > 0.5, ex, ex - 1) + 127
    byte = np.clip(np.where(amax > 0, byte, 1), 1, 254)
    scaled = (w * np.exp2(127.0 - byte)[:, None, :]).reshape(k, n).astype(np.float32)
    by_word = np.ascontiguousarray(scaled.reshape(k // 512, 128, 4, n).transpose(0, 1, 3, 2))
    if fmt == "e4m3":
        words = by_word.astype(ml_dtypes.float8_e4m3fn).view(np.uint8)
    else:
        c = by_word.astype(ml_dtypes.float4_e2m1fn).view(np.uint8) & 0xF
        words = (c[..., 0::2] | (c[..., 1::2] << 4)).reshape(k // 512, 128, 2 * n)
    return np.ascontiguousarray(words), np.ascontiguousarray(byte.astype(np.uint8).reshape(k // 512, 16, n))


def unpack_weight(words, scales, fmt):
    g, _, n = scales.shape
    words = np.ascontiguousarray(words).reshape(g, 128, n, -1)
    if fmt == "e4m3":
        vals = words.view(ml_dtypes.float8_e4m3fn).astype(np.float64)
    else:
        nib = np.empty((g, 128, n, 4), np.uint8)
        nib[..., 0::2] = words & 0xF
        nib[..., 1::2] = words >> 4
        vals = E2M1[nib]
    vals = vals * np.repeat(np.exp2(scales.astype(np.float64) - 127.0), 8, axis=1)[..., None]
    return vals.transpose(0, 1, 3, 2).reshape(g * 512, n)


def pack_table4(v):
    words, scales = pack_weight(v, "e2m1")
    g, t = words.shape[0] // 2, v.shape[1]
    return np.ascontiguousarray(words.reshape(g, 2, 128, t, 2).transpose(0, 2, 3, 1, 4).reshape(g, 128, t, 4)), scales


def unpack_table4(words, scales):
    g, _, t, _ = words.shape
    return unpack_weight(words.reshape(g, 128, t, 2, 2).transpose(0, 3, 1, 2, 4).reshape(2 * g, 128, 2 * t), scales, "e2m1")


def sigm(f):
    return 1.0 / (1.0 + np.exp(-np.maximum(f, -700.0)))


K, L, R, N, T, J = 512, 1024, 512, 512, 2048, 1024


def setup_inputs():
    n = np.random.standard_normal
    s = mx_kscale(K)[:, None]
    s2 = mx_kscale(L)[:, None]
    u = mx_kscale(R)[:, None]
    p_tab = pack_table4(n((L, T)) * s2)
    p_wd = pack_weight(n((R, N)) / np.sqrt(R) / u, "e2m1")
    return {
        "tab_words": p_tab[0],
        "tab_scales": p_tab[1],
        "xT": (n((K, T)) * s).astype(np.float32),
        "wgt2": np.repeat(np.random.uniform(0.5, 2.0, (8, J)), 16, axis=0).astype(np.float32),
        "wa": (n((K, R)) / np.sqrt(K) / s * u.T).astype(np.float32),
        "wb": (n((L, R)) / np.sqrt(L) / s2).astype(np.float32),
        "wd_words": p_wd[0],
        "wd_scales": p_wd[1],
        "b": (0.3 * n(N)).astype(np.float32),
        "offs": striped(np.random.permutation(T)[:J]),
        "offs2": striped8(np.stack([np.random.permutation(T)[:J] for _ in range(8)])),
    }


def reference(tab_words, tab_scales, xT, wgt2, wa, wb, wd_words, wd_scales, b, offs, offs2):
    idx = unstriped(offs)
    idx2 = unstriped8(offs2)
    tab_ = unpack_table4(tab_words, tab_scales)[:, idx]
    rows = np.arange(K)
    xg = f64(wgt2)[rows // 4 % 128] * f64(xT)[rows[:, None], idx2[rows % 512 // 64]]
    xT_ = mxq(xg, 0, "e4m3")
    wa_ = mxq(f64(wa), 0, "e4m3")
    wb_ = mxq(f64(wb), 0, "e4m3")
    ya = wa_.T @ xT_
    yb = wb_.T @ tab_
    h = ya * sigm(yb)
    h_ = mxq(h, 0, "e4m3")
    wd_ = unpack_weight(wd_words, wd_scales, "e2m1")
    y = wd_.T @ h_
    return y + f64(b)[:, None]

@@ -1,0 +1,226 @@
+from contextlib import ExitStack
+
+import concourse.mybir as mybir
+
+K, L, R, N, T, J = 512, 1024, 512, 512, 2048, 1024
+FLOPS = 2 * J * (K * R + L * R + R * N)
+
+F32 = mybir.dt.float32
+BF16 = mybir.dt.bfloat16
+I32 = mybir.dt.int32
+U32 = mybir.dt.uint32
+U16 = mybir.dt.uint16
+U8 = mybir.dt.uint8
+FP8X4 = mybir.dt.float8_e4m3fn_x4
+FP4X4 = mybir.dt.float4_e2m1fn_x4
+MULT = mybir.AluOpType.mult
+SIGMOID = mybir.ActivationFunctionType.Sigmoid
+IDENTITY = mybir.ActivationFunctionType.Identity
+
+P = 128
+PACK = 4
+CH = 128
+NCH = J // CH
+LIST_GROUP = 16
+
+
+def tile_list_htabg_gate_bias_kernel(tc, tab_words, tab_scales, xT, wgt2, wa, wb, wd_words, wd_scales, b, offs, offs2, out):
+    nc = tc.nc
+    with ExitStack() as ctx:
+        keep = ctx.enter_context(tc.tile_pool(name="keep", bufs=1))
+        psum = ctx.enter_context(tc.psum_pool(name="psum", bufs=4))
+
+        def tile(shape, dtype, name):
+            return keep.tile(shape, dtype, name=name, align_bytes=64)
+
+        idx = keep.tile([P, J // LIST_GROUP], U16, name="idx")
+        idx2 = keep.tile([P, J // LIST_GROUP], U16, name="idx2")
+        ts_win = tile([P, T // 4], I32, "ts_win")
+        tw_win = tile([P, T], I32, "tw_win")
+        ts_got = tile([P, J], U8, "ts_got")
+        ts_one = tile([P, J // 4], I32, "ts_one")
+        tw_got = tile([P, J], U32, "tw_got")
+        t_codes = tile([P, 2, J], U16, "t_codes")
+        x_pl = [tile([P, T], F32, "x_pl%d" % i) for i in range(PACK)]
+        wgt = tile([P, J], F32, "wgt")
+        x_got = tile([P, PACK, J], F32, "x_got")
+        x_bf = tile([P, J, PACK], BF16, "x_bf")
+        x_codes = tile([P, J], U32, "x_codes")
+        x_scales = tile([P, J], U8, "x_scales")
+        w_raw = [tile([P, PACK, R], F32, "w_raw%d" % d) for d in range(3)]
+        w_bf = [tile([P, PACK, P, PACK], BF16, "w_bf%d" % d) for d in range(3)]
+        w_codes = [tile([P, R], U32, "w_codes%d" % d) for d in range(3)]
+        w_scales = [tile([P, R], U8, "w_scales%d" % d) for d in range(3)]
+        wd_codes = tile([P, N // 2], I32, "wd_codes")
+        wd_plane = tile([P, N // 4], I32, "wd_plane")
+        bias = tile([P, N // P], F32, "bias")
+        gate = tile([P, J, PACK], F32, "gate")
+        h_bf = tile([P, J, PACK], BF16, "h_bf")
+        h_codes = tile([P, J], U32, "h_codes")
+        h_scales = tile([P, J], U8, "h_scales")
+        y_sb = tile([P, N // P, J], F32, "y_sb")
+
+        nc.vector.memset(ts_win[:], 0)
+        nc.vector.memset(ts_one[:], 0)
+        nc.vector.memset(wd_plane[:], 0)
+
+        def w_rows(src):
+            return src.rearrange("(p i) c -> p i c", i=PACK)
+
+        nc.sync.dma_start(idx[:], offs)
+        nc.sync.dma_start(tw_win[:], tab_words[0].rearrange("p t e -> p (t e)").bitcast(I32))
+        nc.sync.dma_start(w_raw[1][:], w_rows(wb[0:512, :]))
+        for q in range(4):
+            nc.sync.dma_start(ts_win[32 * q : 32 * q + 8, :], tab_scales[:, 4 * q : 4 * q + 4, :].bitcast(I32))
+        nc.sync.dma_start(w_raw[2][:], w_rows(wb[512:1024, :]))
+        nc.sync.dma_start(idx2[:], offs2)
+        nc.sync.dma_start(wgt[:], wgt2)
+        x_rows = xT.rearrange("(p i) t -> p i t", i=PACK)
+        for i in range(PACK):
+            nc.sync.dma_start(x_pl[i][:], x_rows[:, i, :])
+        nc.sync.dma_start(w_raw[0][:], w_rows(wa))
+        nc.sync.dma_start(wd_codes[:], wd_words[0].bitcast(I32))
+        for q in range(4):
+            nc.sync.dma_start(wd_plane[32 * q : 32 * q + 4, :], wd_scales[0, 4 * q : 4 * q + 4, :].bitcast(I32))
+        with nc.allow_non_contiguous_dma(reason="one bias value for each partition"):
+            nc.sync.dma_start(bias[:], b.rearrange("(a p) -> p a", p=P))
+
+        def entries(lst, j0, j1):
+            return lst[:, j0 // LIST_GROUP : j1 // LIST_GROUP]
+
+        def cast_w(copy, d, m0, m1):
+            copy(
+                w_bf[d][:, :, m0:m1, :].rearrange("p t m i -> p m i t"),
+                w_raw[d][:, :, PACK * m0 : PACK * m1].rearrange("p i (m t) -> p m i t", t=PACK),
+            )
+
+        def quantize(codes, scales, src):
+            nc.vector.quantize_mx(out=codes.bitcast(FP8X4), scales=scales, in_=src)
+
+        def quantize_w(d):
+            quantize(w_codes[d][:], w_scales[d][:], w_bf[d][:].rearrange("p t m i -> p (t m i)"))
+
+        half = J // 2
+        for j0 in (0, half):
+            nc.vector.tensor_copy(tw_got[:, j0 : j0 + half], tw_win[:].bitcast(U32).indirect(entries(idx, j0, j0 + half)))
+        cast_w(nc.scalar.copy, 1, 0, P)
+        cast_w(nc.scalar.copy, 2, 0, P)
+        for j0 in (0, half):
+            nc.vector.tensor_copy(ts_got[:, j0 : j0 + half], ts_win[:].bitcast(U8).indirect(entries(idx, j0, j0 + half)))
+            nc.gpsimd.dma_start(
+                ts_one[0:112, j0 // 4 : (j0 + half) // 4], ts_got[4:116, j0 : j0 + half].bitcast(I32)
+            )
+        for j0 in (0, half):
+            nc.vector.tensor_copy(
+                t_codes[:, :, j0 : j0 + half],
+                tw_got[:, j0 : j0 + half].bitcast(U16).rearrange("p (n d) -> p d n", d=2),
+            )
+        quantize_w(1)
+        quantize_w(2)
+        t_planes = [ts_got[:], ts_one[:].bitcast(U8)]
+
+        for c in range(NCH):
+            js = slice(c * CH, (c + 1) * CH)
+            acc = psum.tile([P, PACK, CH], F32, name="acc")
+            for t in range(PACK):
+                ms = slice(t * P, (t + 1) * P)
+                for d in range(2):
+                    nc.tensor.matmul_mx(
+                        out=acc[:, t, :],
+                        lhsT=w_codes[1 + d][:, ms].bitcast(FP8X4),
+                        lhsT_scale=w_scales[1 + d][:, ms],
+                        rhs=t_codes[:, d, js].bitcast(FP4X4),
+                        rhs_scale=t_planes[d][:, js],
+                        start=(d == 0),
+                        stop=(d == 1),
+                    )
+            nc.scalar.activation(gate[:, js, :], acc[:].rearrange("p t n -> p n t"), SIGMOID)
+
+        def gather_x(i, j0, j1):
+            nc.vector.tensor_tensor(x_got[:, i, j0:j1], x_pl[i][:].indirect(entries(idx2, j0, j1)), wgt[:, j0:j1], MULT)
+
+        for i in range(PACK - 1):
+            for j0 in (0, half):
+                gather_x(i, j0, j0 + half)
+
+        def round_x(j0, j1):
+            nc.scalar.copy(
+                x_bf[:, j0:j1, :].rearrange("p (c u) i -> p c i u", u=4),
+                x_got[:, :, j0:j1].rearrange("p i (c u) -> p c i u", u=4),
+            )
+
+        def quantize_x(j0, j1):
+            quantize(x_codes[:, j0:j1], x_scales[:, j0:j1], x_bf[:, j0:j1, :].rearrange("p n i -> p (n i)"))
+
+        quarter = J // 4
+        for j0 in range(0, J, quarter):
+            gather_x(PACK - 1, j0, j0 + quarter)
+        round_x(0, quarter)
+        quantize_x(0, quarter)
+        cast_w(nc.scalar.copy, 0, 0, P // 2)
+        cast_w(nc.vector.tensor_copy, 0, P // 2, P)
+        quantize_w(0)
+        round_x(quarter, 2 * quarter)
+        quantize_x(quarter, 2 * quarter)
+
+        def gated(c):
+            js = slice(c * CH, (c + 1) * CH)
+            acc = psum.tile([P, PACK, CH], F32, name="acc")
+            for t in range(PACK):
+                ms = slice(t * P, (t + 1) * P)
+                nc.tensor.matmul_mx(
+                    out=acc[:, t, :],
+                    lhsT=w_codes[0][:, ms].bitcast(FP8X4),
+                    lhsT_scale=w_scales[0][:, ms],
+                    rhs=x_codes[:, js].bitcast(FP8X4),
+                    rhs_scale=x_scales[:, js],
+                    start=True,
+                    stop=True,
+                )
+            nc.vector.tensor_tensor(h_bf[:, js, :], acc[:].rearrange("p t n -> p n t"), gate[:, js, :], MULT)
+
+        out_v = out.rearrange("(a p) j -> p a j", p=P)
+        wd_u8 = wd_codes[:].bitcast(U8)
+        wd_pl = wd_plane[:].bitcast(U8)
+
+        def second(j0, j1, share):
+            w = j1 - j0
+            quantize(h_codes[:, j0:j1], h_scales[:, j0:j1], h_bf[:, j0:j1, :].rearrange("p n i -> p (n i)"))
+            for pair in range(2):
+                yacc = psum.tile([P, 2, 256], F32, name="yacc")
+                for s in range(2):
+                    a = 2 * pair + s
+                    nc.tensor.matmul_mx(
+                        out=yacc[:, s, 0:w],
+                        lhsT=wd_u8[:, 2 * P * a : 2 * P * (a + 1)].bitcast(FP4X4),
+                        lhsT_scale=wd_pl[:, P * a : P * (a + 1)],
+                        rhs=h_codes[:, j0:j1].bitcast(FP8X4),
+                        rhs_scale=h_scales[:, j0:j1],
+                        start=True,
+                        stop=True,
+                    )
+                for s in range(2):
+                    a = 2 * pair + s
+                    if share and pair == 1:
+                        nc.vector.tensor_scalar_add(y_sb[:, a, j0:j1], yacc[:, s, 0:w], bias[:, a : a + 1])
+                    else:
+                        nc.scalar.activation(y_sb[:, a, j0:j1], yacc[:, s, 0:w], IDENTITY, bias=bias[:, a : a + 1])
+            nc.sync.dma_start(out_v[:, :, j0:j1], y_sb[:, :, j0:j1])
+
+        gated(0)
+        gated(1)
+        round_x(2 * quarter, 3 * quarter)
+        quantize_x(2 * quarter, 3 * quarter)
+        gated(2)
+        second(0, 256, False)
+        round_x(3 * quarter, J)
+        quantize_x(3 * quarter, J)
+        gated(3)
+        gated(4)
+        second(256, 512, False)
+        gated(5)
+        gated(6)
+        second(512, 768, False)
+        gated(7)
+        second(768, 896, False)
+        second(896, 1024, True)

@@ -35,15 +35,14 @@ def tile_list_htabg_gate_bias_kernel(tc, tab_words, tab_scales, xT, wgt2, wa, wb
 
         idx = keep.tile([P, J // LIST_GROUP], U16, name="idx")
         idx2 = keep.tile([P, J // LIST_GROUP], U16, name="idx2")
-        ts_win = tile([P, T // 4], I32, "ts_win")
+        ts_win = tile([P, 2, T // 4], I32, "ts_win")
         tw_win = tile([P, T], I32, "tw_win")
-        ts_got = tile([P, J], U8, "ts_got")
-        ts_one = tile([P, J // 4], I32, "ts_one")
+        ts_got = tile([P, 2, J], U8, "ts_got")
         tw_got = tile([P, J], U32, "tw_got")
-        t_codes = tile([P, 2, J], U16, "t_codes")
+        t_codes = [tile([P, 2, J // 2], U16, "t_codes%d" % h) for h in range(2)]
         x_pl = [tile([P, T], F32, "x_pl%d" % i) for i in range(PACK)]
         wgt = tile([P, J], F32, "wgt")
-        x_got = tile([P, PACK, J], F32, "x_got")
+        x_got = [tile([P, PACK, J // 2], F32, "x_got%d" % h) for h in range(2)]
         x_bf = tile([P, J, PACK], BF16, "x_bf")
         x_codes = tile([P, J], U32, "x_codes")
         x_scales = tile([P, J], U8, "x_scales")
@@ -58,27 +57,31 @@ def tile_list_htabg_gate_bias_kernel(tc, tab_words, tab_scales, xT, wgt2, wa, wb
         h_bf = tile([P, J, PACK], BF16, "h_bf")
         h_codes = tile([P, J], U32, "h_codes")
         h_scales = tile([P, J], U8, "h_scales")
-        y_sb = tile([P, N // P, J], F32, "y_sb")
 
-        nc.vector.memset(ts_win[:], 0)
-        nc.vector.memset(ts_one[:], 0)
+        nc.vector.memset(ts_win[:, 0, :], 0)
+        nc.gpsimd.memset(ts_win[:, 1, :], 0)
         nc.vector.memset(wd_plane[:], 0)
 
         def w_rows(src):
             return src.rearrange("(p i) c -> p i c", i=PACK)
 
         nc.sync.dma_start(idx[:], offs)
-        nc.sync.dma_start(tw_win[:], tab_words[0].rearrange("p t e -> p (t e)").bitcast(I32))
-        nc.sync.dma_start(w_raw[1][:], w_rows(wb[0:512, :]))
-        for q in range(4):
-            nc.sync.dma_start(ts_win[32 * q : 32 * q + 8, :], tab_scales[:, 4 * q : 4 * q + 4, :].bitcast(I32))
-        nc.sync.dma_start(w_raw[2][:], w_rows(wb[512:1024, :]))
         nc.sync.dma_start(idx2[:], offs2)
         nc.sync.dma_start(wgt[:], wgt2)
+        for q in range(4):
+            nc.sync.dma_start(
+                ts_win[32 * q : 32 * q + 4, :, :],
+                tab_scales[:, 4 * q : 4 * q + 4, :].rearrange("a r t -> r a t").bitcast(I32),
+            )
+        nc.sync.dma_start(tw_win[:], tab_words[0].rearrange("p t e -> p (t e)").bitcast(I32))
+        nc.sync.dma_start(w_raw[1][:], w_rows(wb[0:512, :]))
+        nc.sync.dma_start(w_raw[2][:], w_rows(wb[512:1024, :]))
         x_rows = xT.rearrange("(p i) t -> p i t", i=PACK)
-        for i in range(PACK):
-            nc.sync.dma_start(x_pl[i][:], x_rows[:, i, :])
+        nc.sync.dma_start(x_pl[0][:], x_rows[:, 0, :])
+        nc.sync.dma_start(x_pl[1][:], x_rows[:, 1, :])
         nc.sync.dma_start(w_raw[0][:], w_rows(wa))
+        nc.sync.dma_start(x_pl[2][:], x_rows[:, 2, :])
+        nc.sync.dma_start(x_pl[3][:], x_rows[:, 3, :])
         nc.sync.dma_start(wd_codes[:], wd_words[0].bitcast(I32))
         for q in range(4):
             nc.sync.dma_start(wd_plane[32 * q : 32 * q + 4, :], wd_scales[0, 4 * q : 4 * q + 4, :].bitcast(I32))
@@ -88,36 +91,36 @@ def tile_list_htabg_gate_bias_kernel(tc, tab_words, tab_scales, xT, wgt2, wa, wb
         def entries(lst, j0, j1):
             return lst[:, j0 // LIST_GROUP : j1 // LIST_GROUP]
 
-        def cast_w(copy, d, m0, m1):
+        def cast_w(copy, d, t0, t1):
             copy(
-                w_bf[d][:, :, m0:m1, :].rearrange("p t m i -> p m i t"),
-                w_raw[d][:, :, PACK * m0 : PACK * m1].rearrange("p i (m t) -> p m i t", t=PACK),
+                w_bf[d][:, t0:t1, :, :].rearrange("p t m i -> p m i t"),
+                w_raw[d][:].rearrange("p i (m t) -> p m i t", t=PACK)[:, :, :, t0:t1],
             )
 
         def quantize(codes, scales, src):
             nc.vector.quantize_mx(out=codes.bitcast(FP8X4), scales=scales, in_=src)
 
-        def quantize_w(d):
-            quantize(w_codes[d][:], w_scales[d][:], w_bf[d][:].rearrange("p t m i -> p (t m i)"))
+        def quantize_w(d, t0, t1):
+            ms = slice(t0 * P, t1 * P)
+            quantize(w_codes[d][:, ms], w_scales[d][:, ms], w_bf[d][:, t0:t1, :, :].rearrange("p t m i -> p (t m i)"))
 
         half = J // 2
         for j0 in (0, half):
+            for a in range(2):
+                nc.vector.tensor_copy(
+                    ts_got[:, a, j0 : j0 + half], ts_win[:, a, :].bitcast(U8).indirect(entries(idx, j0, j0 + half))
+                )
+        for j0 in (0, half):
             nc.vector.tensor_copy(tw_got[:, j0 : j0 + half], tw_win[:].bitcast(U32).indirect(entries(idx, j0, j0 + half)))
-        cast_w(nc.scalar.copy, 1, 0, P)
-        cast_w(nc.scalar.copy, 2, 0, P)
-        for j0 in (0, half):
-            nc.vector.tensor_copy(ts_got[:, j0 : j0 + half], ts_win[:].bitcast(U8).indirect(entries(idx, j0, j0 + half)))
-            nc.gpsimd.dma_start(
-                ts_one[0:112, j0 // 4 : (j0 + half) // 4], ts_got[4:116, j0 : j0 + half].bitcast(I32)
-            )
-        for j0 in (0, half):
+        cast_w(nc.scalar.copy, 1, 0, PACK)
+        cast_w(nc.scalar.copy, 2, 0, PACK)
+        for h in range(2):
             nc.vector.tensor_copy(
-                t_codes[:, :, j0 : j0 + half],
-                tw_got[:, j0 : j0 + half].bitcast(U16).rearrange("p (n d) -> p d n", d=2),
+                t_codes[h][:],
+                tw_got[:, h * half : (h + 1) * half].bitcast(U16).rearrange("p (n d) -> p d n", d=2),
             )
-        quantize_w(1)
-        quantize_w(2)
-        t_planes = [ts_got[:], ts_one[:].bitcast(U8)]
+        quantize_w(1, 0, PACK)
+        quantize_w(2, 0, PACK)
 
         for c in range(NCH):
             js = slice(c * CH, (c + 1) * CH)
@@ -129,39 +132,37 @@ def tile_list_htabg_gate_bias_kernel(tc, tab_words, tab_scales, xT, wgt2, wa, wb
                         out=acc[:, t, :],
                         lhsT=w_codes[1 + d][:, ms].bitcast(FP8X4),
                         lhsT_scale=w_scales[1 + d][:, ms],
-                        rhs=t_codes[:, d, js].bitcast(FP4X4),
-                        rhs_scale=t_planes[d][:, js],
+                        rhs=t_codes[c // 4][:, d, (c % 4) * CH : (c % 4 + 1) * CH].bitcast(FP4X4),
+                        rhs_scale=ts_got[:, d, js],
                         start=(d == 0),
                         stop=(d == 1),
                     )
             nc.scalar.activation(gate[:, js, :], acc[:].rearrange("p t n -> p n t"), SIGMOID)
 
         def gather_x(i, j0, j1):
-            nc.vector.tensor_tensor(x_got[:, i, j0:j1], x_pl[i][:].indirect(entries(idx2, j0, j1)), wgt[:, j0:j1], MULT)
+            nc.vector.tensor_tensor(x_got[j0 // half][:, i, j0 % half : j0 % half + j1 - j0], x_pl[i][:].indirect(entries(idx2, j0, j1)), wgt[:, j0:j1], MULT)
 
+        cast_w(nc.scalar.copy, 0, 0, PACK)
         for i in range(PACK - 1):
             for j0 in (0, half):
                 gather_x(i, j0, j0 + half)
+        quantize_w(0, 0, PACK)
 
         def round_x(j0, j1):
             nc.scalar.copy(
                 x_bf[:, j0:j1, :].rearrange("p (c u) i -> p c i u", u=4),
-                x_got[:, :, j0:j1].rearrange("p i (c u) -> p c i u", u=4),
+                x_got[j0 // half][:, :, j0 % half : j0 % half + j1 - j0].rearrange("p i (c u) -> p c i u", u=4),
             )
 
         def quantize_x(j0, j1):
             quantize(x_codes[:, j0:j1], x_scales[:, j0:j1], x_bf[:, j0:j1, :].rearrange("p n i -> p (n i)"))
 
-        quarter = J // 4
-        for j0 in range(0, J, quarter):
-            gather_x(PACK - 1, j0, j0 + quarter)
-        round_x(0, quarter)
-        quantize_x(0, quarter)
-        cast_w(nc.scalar.copy, 0, 0, P // 2)
-        cast_w(nc.vector.tensor_copy, 0, P // 2, P)
-        quantize_w(0)
-        round_x(quarter, 2 * quarter)
-        quantize_x(quarter, 2 * quarter)
+        pieces = [(0, 128), (128, 256), (256, 512), (512, 768), (768, 1024)]
+        for j0, j1 in pieces:
+            gather_x(PACK - 1, j0, j1)
+        for j0, j1 in pieces:
+            round_x(j0, j1)
+            quantize_x(j0, j1)
 
         def gated(c):
             js = slice(c * CH, (c + 1) * CH)
@@ -185,6 +186,7 @@ def tile_list_htabg_gate_bias_kernel(tc, tab_words, tab_scales, xT, wgt2, wa, wb
 
         def second(j0, j1, share):
             w = j1 - j0
+            y_sb = tile([P, N // P, w], F32, "y_sb%d" % j0)
             quantize(h_codes[:, j0:j1], h_scales[:, j0:j1], h_bf[:, j0:j1, :].rearrange("p n i -> p (n i)"))
             for pair in range(2):
                 yacc = psum.tile([P, 2, 256], F32, name="yacc")
@@ -202,19 +204,15 @@ def tile_list_htabg_gate_bias_kernel(tc, tab_words, tab_scales, xT, wgt2, wa, wb
                 for s in range(2):
                     a = 2 * pair + s
                     if share and pair == 1:
-                        nc.vector.tensor_scalar_add(y_sb[:, a, j0:j1], yacc[:, s, 0:w], bias[:, a : a + 1])
+                        nc.vector.tensor_scalar_add(y_sb[:, a, :], yacc[:, s, 0:w], bias[:, a : a + 1])
                     else:
-                        nc.scalar.activation(y_sb[:, a, j0:j1], yacc[:, s, 0:w], IDENTITY, bias=bias[:, a : a + 1])
-            nc.sync.dma_start(out_v[:, :, j0:j1], y_sb[:, :, j0:j1])
+                        nc.scalar.activation(y_sb[:, a, :], yacc[:, s, 0:w], IDENTITY, bias=bias[:, a : a + 1])
+            nc.sync.dma_start(out_v[:, :, j0:j1], y_sb[:])
 
         gated(0)
         gated(1)
-        round_x(2 * quarter, 3 * quarter)
-        quantize_x(2 * quarter, 3 * quarter)
         gated(2)
         second(0, 256, False)
-        round_x(3 * quarter, J)
-        quantize_x(3 * quarter, J)
         gated(3)
         gated(4)
         second(256, 512, False)

@@ -14,6 +14,7 @@ U8 = mybir.dt.uint8
 FP8X4 = mybir.dt.float8_e4m3fn_x4
 FP4X4 = mybir.dt.float4_e2m1fn_x4
 MULT = mybir.AluOpType.mult
+ADD = mybir.AluOpType.add
 SIGMOID = mybir.ActivationFunctionType.Sigmoid
 IDENTITY = mybir.ActivationFunctionType.Identity
 
@@ -35,9 +36,10 @@ def tile_list_htabg_gate_bias_kernel(tc, tab_words, tab_scales, xT, wgt2, wa, wb
 
         idx = keep.tile([P, J // LIST_GROUP], U16, name="idx")
         idx2 = keep.tile([P, J // LIST_GROUP], U16, name="idx2")
-        ts_win = tile([P, 2, T // 4], I32, "ts_win")
+        ts_win = tile([P, T // 4], I32, "ts_win")
         tw_win = tile([P, T], I32, "tw_win")
-        ts_got = tile([P, 2, J], U8, "ts_got")
+        ts_got = tile([P, J], U8, "ts_got")
+        ts_one = tile([P, J // 4], I32, "ts_one")
         tw_got = tile([P, J], U32, "tw_got")
         t_codes = [tile([P, 2, J // 2], U16, "t_codes%d" % h) for h in range(2)]
         x_pl = [tile([P, T], F32, "x_pl%d" % i) for i in range(PACK)]
@@ -58,33 +60,33 @@ def tile_list_htabg_gate_bias_kernel(tc, tab_words, tab_scales, xT, wgt2, wa, wb
         h_codes = tile([P, J], U32, "h_codes")
         h_scales = tile([P, J], U8, "h_scales")
 
-        nc.vector.memset(ts_win[:, 0, :], 0)
-        nc.gpsimd.memset(ts_win[:, 1, :], 0)
+        nc.vector.memset(ts_win[:], 0)
+        nc.vector.memset(ts_one[:], 0)
         nc.vector.memset(wd_plane[:], 0)
 
         def w_rows(src):
             return src.rearrange("(p i) c -> p i c", i=PACK)
 
+        x_rows = xT.rearrange("(p i) t -> p i t", i=PACK)
+        nc.sync.dma_start(tw_win[:], tab_words[0].rearrange("p t e -> p (t e)").bitcast(I32))
         nc.sync.dma_start(idx[:], offs)
         nc.sync.dma_start(idx2[:], offs2)
-        nc.sync.dma_start(wgt[:], wgt2)
         for q in range(4):
-            nc.sync.dma_start(
-                ts_win[32 * q : 32 * q + 4, :, :],
-                tab_scales[:, 4 * q : 4 * q + 4, :].rearrange("a r t -> r a t").bitcast(I32),
-            )
-        nc.sync.dma_start(tw_win[:], tab_words[0].rearrange("p t e -> p (t e)").bitcast(I32))
+            nc.sync.dma_start(ts_win[32 * q : 32 * q + 8, :], tab_scales[:, 4 * q : 4 * q + 4, :].bitcast(I32))
         nc.sync.dma_start(w_raw[1][:], w_rows(wb[0:512, :]))
         nc.sync.dma_start(w_raw[2][:], w_rows(wb[512:1024, :]))
-        x_rows = xT.rearrange("(p i) t -> p i t", i=PACK)
-        nc.sync.dma_start(x_pl[0][:], x_rows[:, 0, :])
-        nc.sync.dma_start(x_pl[1][:], x_rows[:, 1, :])
-        nc.sync.dma_start(w_raw[0][:], w_rows(wa))
-        nc.sync.dma_start(x_pl[2][:], x_rows[:, 2, :])
-        nc.sync.dma_start(x_pl[3][:], x_rows[:, 3, :])
-        nc.sync.dma_start(wd_codes[:], wd_words[0].bitcast(I32))
+        nc.sync.dma_start(wgt[:, 0 : J // 2], wgt2[:, 0 : J // 2])
+        nc.sync.dma_start(wgt[:, J // 2 : J], wgt2[:, J // 2 : J])
         for q in range(4):
             nc.sync.dma_start(wd_plane[32 * q : 32 * q + 4, :], wd_scales[0, 4 * q : 4 * q + 4, :].bitcast(I32))
+        nc.sync.dma_start(x_pl[0][:], x_rows[:, 0, :])
+        nc.vector.tensor_copy(ts_got[:], ts_win[:].bitcast(U8).indirect(idx[:]))
+        nc.sync.dma_start(ts_one[0:112, :], ts_got[4:116, :].bitcast(I32))
+        nc.sync.dma_start(x_pl[1][:], x_rows[:, 1, :])
+        nc.sync.dma_start(x_pl[2][:], x_rows[:, 2, :])
+        nc.sync.dma_start(x_pl[3][:], x_rows[:, 3, :])
+        nc.sync.dma_start(w_raw[0][:], w_rows(wa))
+        nc.sync.dma_start(wd_codes[:], wd_words[0].bitcast(I32))
         with nc.allow_non_contiguous_dma(reason="one bias value for each partition"):
             nc.sync.dma_start(bias[:], b.rearrange("(a p) -> p a", p=P))
 
@@ -105,11 +107,7 @@ def tile_list_htabg_gate_bias_kernel(tc, tab_words, tab_scales, xT, wgt2, wa, wb
             quantize(w_codes[d][:, ms], w_scales[d][:, ms], w_bf[d][:, t0:t1, :, :].rearrange("p t m i -> p (t m i)"))
 
         half = J // 2
-        for j0 in (0, half):
-            for a in range(2):
-                nc.vector.tensor_copy(
-                    ts_got[:, a, j0 : j0 + half], ts_win[:, a, :].bitcast(U8).indirect(entries(idx, j0, j0 + half))
-                )
+        t_planes = [ts_got[:], ts_one[:].bitcast(U8)]
         for j0 in (0, half):
             nc.vector.tensor_copy(tw_got[:, j0 : j0 + half], tw_win[:].bitcast(U32).indirect(entries(idx, j0, j0 + half)))
         cast_w(nc.scalar.copy, 1, 0, PACK)
@@ -133,7 +131,7 @@ def tile_list_htabg_gate_bias_kernel(tc, tab_words, tab_scales, xT, wgt2, wa, wb
                         lhsT=w_codes[1 + d][:, ms].bitcast(FP8X4),
                         lhsT_scale=w_scales[1 + d][:, ms],
                         rhs=t_codes[c // 4][:, d, (c % 4) * CH : (c % 4 + 1) * CH].bitcast(FP4X4),
-                        rhs_scale=ts_got[:, d, js],
+                        rhs_scale=t_planes[d][:, js],
                         start=(d == 0),
                         stop=(d == 1),
                     )
@@ -142,27 +140,14 @@ def tile_list_htabg_gate_bias_kernel(tc, tab_words, tab_scales, xT, wgt2, wa, wb
         def gather_x(i, j0, j1):
             nc.vector.tensor_tensor(x_got[j0 // half][:, i, j0 % half : j0 % half + j1 - j0], x_pl[i][:].indirect(entries(idx2, j0, j1)), wgt[:, j0:j1], MULT)
 
-        cast_w(nc.scalar.copy, 0, 0, PACK)
-        for i in range(PACK - 1):
-            for j0 in (0, half):
-                gather_x(i, j0, j0 + half)
-        quantize_w(0, 0, PACK)
-
-        def round_x(j0, j1):
-            nc.scalar.copy(
-                x_bf[:, j0:j1, :].rearrange("p (c u) i -> p c i u", u=4),
-                x_got[j0 // half][:, :, j0 % half : j0 % half + j1 - j0].rearrange("p i (c u) -> p c i u", u=4),
+        def round_x(j0, j1, i0, i1, copy=nc.scalar.copy):
+            copy(
+                x_bf[:, j0:j1, i0:i1].rearrange("p (c u) i -> p c i u", u=4),
+                x_got[j0 // half][:, i0:i1, j0 % half : j0 % half + j1 - j0].rearrange("p i (c u) -> p c i u", u=4),
             )
 
         def quantize_x(j0, j1):
             quantize(x_codes[:, j0:j1], x_scales[:, j0:j1], x_bf[:, j0:j1, :].rearrange("p n i -> p (n i)"))
-
-        pieces = [(0, 128), (128, 256), (256, 512), (512, 768), (768, 1024)]
-        for j0, j1 in pieces:
-            gather_x(PACK - 1, j0, j1)
-        for j0, j1 in pieces:
-            round_x(j0, j1)
-            quantize_x(j0, j1)
 
         def gated(c):
             js = slice(c * CH, (c + 1) * CH)
@@ -184,16 +169,19 @@ def tile_list_htabg_gate_bias_kernel(tc, tab_words, tab_scales, xT, wgt2, wa, wb
         wd_u8 = wd_codes[:].bitcast(U8)
         wd_pl = wd_plane[:].bitcast(U8)
 
-        def second(j0, j1, share):
-            w = j1 - j0
-            y_sb = tile([P, N // P, w], F32, "y_sb%d" % j0)
+        def quantize_h(j0, j1):
             quantize(h_codes[:, j0:j1], h_scales[:, j0:j1], h_bf[:, j0:j1, :].rearrange("p n i -> p (n i)"))
-            for pair in range(2):
-                yacc = psum.tile([P, 2, 256], F32, name="yacc")
-                for s in range(2):
-                    a = 2 * pair + s
+
+        def second(j0, j1, who, split=False):
+            w = j1 - j0
+            per = 4 // len(who)
+            y_sb = tile([P, N // P, w], F32, "y_sb%d" % j0)
+            for g in range(4 // per):
+                yacc = psum.tile([P, per, w], F32, name="yacc")
+                for s in range(per):
+                    a = per * g + s
                     nc.tensor.matmul_mx(
-                        out=yacc[:, s, 0:w],
+                        out=yacc[:, s, :],
                         lhsT=wd_u8[:, 2 * P * a : 2 * P * (a + 1)].bitcast(FP4X4),
                         lhsT_scale=wd_pl[:, P * a : P * (a + 1)],
                         rhs=h_codes[:, j0:j1].bitcast(FP8X4),
@@ -201,24 +189,53 @@ def tile_list_htabg_gate_bias_kernel(tc, tab_words, tab_scales, xT, wgt2, wa, wb
                         start=True,
                         stop=True,
                     )
-                for s in range(2):
-                    a = 2 * pair + s
-                    if share and pair == 1:
-                        nc.vector.tensor_scalar_add(y_sb[:, a, :], yacc[:, s, 0:w], bias[:, a : a + 1])
-                    else:
-                        nc.scalar.activation(y_sb[:, a, :], yacc[:, s, 0:w], IDENTITY, bias=bias[:, a : a + 1])
-            nc.sync.dma_start(out_v[:, :, j0:j1], y_sb[:])
+                sel = slice(per * g, per * (g + 1))
+                if who[g] == "V":
+                    nc.vector.tensor_tensor(y_sb[:, sel, :], yacc[:], bias[:, sel].unsqueeze(2).to_broadcast([P, per, w]), ADD)
+                else:
+                    for s in range(per):
+                        a = per * g + s
+                        nc.scalar.activation(y_sb[:, a, :], yacc[:, s, :], IDENTITY, bias=bias[:, a : a + 1])
+                if split:
+                    nc.sync.dma_start(out_v[:, sel, j0:j1], y_sb[:, sel, :])
+            if not split:
+                nc.sync.dma_start(out_v[:, :, j0:j1], y_sb[:])
 
+        gather_x(0, 0, 512)
+        gather_x(0, 512, 1024)
+        gather_x(1, 0, 512)
+        gather_x(1, 512, 1024)
+        gather_x(2, 0, 512)
+        gather_x(2, 512, 1024)
+        cast_w(nc.vector.tensor_copy, 0, 0, 4)
+        quantize_w(0, 0, 4)
+        gather_x(3, 0, 256)
+        round_x(0, 256, 0, 4)
+        quantize_x(0, 256)
+        gather_x(3, 256, 512)
+        round_x(256, 512, 0, 4)
+        gather_x(3, 512, 768)
+        round_x(512, 768, 0, 4)
+        gather_x(3, 768, 1024)
+        round_x(768, 1024, 0, 4)
         gated(0)
         gated(1)
+        quantize_x(256, 512)
+        quantize_x(512, 768)
         gated(2)
-        second(0, 256, False)
+        quantize_h(0, 256)
         gated(3)
         gated(4)
-        second(256, 512, False)
+        second(0, 256, "SS", True)
+        quantize_h(256, 512)
+        quantize_x(768, 1024)
         gated(5)
         gated(6)
-        second(512, 768, False)
+        second(256, 512, "SS", True)
+        quantize_h(512, 768)
         gated(7)
-        second(768, 896, False)
-        second(896, 1024, True)
+        quantize_h(768, 896)
+        quantize_h(896, 1024)
+        second(512, 768, "SS", True)
+        second(768, 896, "V", True)
+        second(896, 1024, "VS", True)

from contextlib import ExitStack

import concourse.mybir as mybir

K, L, R, N, T, J = 512, 1024, 512, 512, 2048, 1024
FLOPS = 2 * J * (K * R + L * R + R * N)

F32 = mybir.dt.float32
BF16 = mybir.dt.bfloat16
I32 = mybir.dt.int32
U32 = mybir.dt.uint32
U16 = mybir.dt.uint16
U8 = mybir.dt.uint8
FP8X4 = mybir.dt.float8_e4m3fn_x4
FP4X4 = mybir.dt.float4_e2m1fn_x4
MULT = mybir.AluOpType.mult
ADD = mybir.AluOpType.add
SIGMOID = mybir.ActivationFunctionType.Sigmoid
IDENTITY = mybir.ActivationFunctionType.Identity

P = 128
PACK = 4
CH = 128
NCH = J // CH
LIST_GROUP = 16


def tile_list_htabg_gate_bias_kernel(tc, tab_words, tab_scales, xT, wgt2, wa, wb, wd_words, wd_scales, b, offs, offs2, out):
    nc = tc.nc
    with ExitStack() as ctx:
        keep = ctx.enter_context(tc.tile_pool(name="keep", bufs=1))
        psum = ctx.enter_context(tc.psum_pool(name="psum", bufs=4))

        def tile(shape, dtype, name):
            return keep.tile(shape, dtype, name=name, align_bytes=64)

        idx = keep.tile([P, J // LIST_GROUP], U16, name="idx")
        idx2 = keep.tile([P, J // LIST_GROUP], U16, name="idx2")
        ts_win = tile([P, T // 4], I32, "ts_win")
        tw_win = tile([P, T], I32, "tw_win")
        ts_got = tile([P, J], U8, "ts_got")
        ts_one = tile([P, J // 4], I32, "ts_one")
        tw_got = tile([P, J], U32, "tw_got")
        t_codes = [tile([P, 2, J // 2], U16, "t_codes%d" % h) for h in range(2)]
        x_pl = [tile([P, T], F32, "x_pl%d" % i) for i in range(PACK)]
        wgt = tile([P, J], F32, "wgt")
        x_got = [tile([P, PACK, J // 2], F32, "x_got%d" % h) for h in range(2)]
        x_bf = tile([P, J, PACK], BF16, "x_bf")
        x_codes = tile([P, J], U32, "x_codes")
        x_scales = tile([P, J], U8, "x_scales")
        w_raw = [tile([P, PACK, R], F32, "w_raw%d" % d) for d in range(3)]
        w_bf = [tile([P, PACK, P, PACK], BF16, "w_bf%d" % d) for d in range(3)]
        w_codes = [tile([P, R], U32, "w_codes%d" % d) for d in range(3)]
        w_scales = [tile([P, R], U8, "w_scales%d" % d) for d in range(3)]
        wd_codes = tile([P, N // 2], I32, "wd_codes")
        wd_plane = tile([P, N // 4], I32, "wd_plane")
        bias = tile([P, N // P], F32, "bias")
        gate = tile([P, J, PACK], F32, "gate")
        h_bf = tile([P, J, PACK], BF16, "h_bf")
        h_codes = tile([P, J], U32, "h_codes")
        h_scales = tile([P, J], U8, "h_scales")

        nc.vector.memset(ts_win[:], 0)
        nc.vector.memset(ts_one[:], 0)
        nc.vector.memset(wd_plane[:], 0)

        def w_rows(src):
            return src.rearrange("(p i) c -> p i c", i=PACK)

        x_rows = xT.rearrange("(p i) t -> p i t", i=PACK)
        nc.sync.dma_start(tw_win[:], tab_words[0].rearrange("p t e -> p (t e)").bitcast(I32))
        nc.sync.dma_start(idx[:], offs)
        nc.sync.dma_start(idx2[:], offs2)
        for q in range(4):
            nc.sync.dma_start(ts_win[32 * q : 32 * q + 8, :], tab_scales[:, 4 * q : 4 * q + 4, :].bitcast(I32))
        nc.sync.dma_start(w_raw[1][:], w_rows(wb[0:512, :]))
        nc.sync.dma_start(w_raw[2][:], w_rows(wb[512:1024, :]))
        nc.sync.dma_start(wgt[:, 0 : J // 2], wgt2[:, 0 : J // 2])
        nc.sync.dma_start(wgt[:, J // 2 : J], wgt2[:, J // 2 : J])
        for q in range(4):
            nc.sync.dma_start(wd_plane[32 * q : 32 * q + 4, :], wd_scales[0, 4 * q : 4 * q + 4, :].bitcast(I32))
        nc.sync.dma_start(x_pl[0][:], x_rows[:, 0, :])
        nc.vector.tensor_copy(ts_got[:], ts_win[:].bitcast(U8).indirect(idx[:]))
        nc.sync.dma_start(ts_one[0:112, :], ts_got[4:116, :].bitcast(I32))
        nc.sync.dma_start(x_pl[1][:], x_rows[:, 1, :])
        nc.sync.dma_start(x_pl[2][:], x_rows[:, 2, :])
        nc.sync.dma_start(x_pl[3][:], x_rows[:, 3, :])
        nc.sync.dma_start(w_raw[0][:], w_rows(wa))
        nc.sync.dma_start(wd_codes[:], wd_words[0].bitcast(I32))
        with nc.allow_non_contiguous_dma(reason="one bias value for each partition"):
            nc.sync.dma_start(bias[:], b.rearrange("(a p) -> p a", p=P))

        def entries(lst, j0, j1):
            return lst[:, j0 // LIST_GROUP : j1 // LIST_GROUP]

        def cast_w(copy, d, t0, t1):
            copy(
                w_bf[d][:, t0:t1, :, :].rearrange("p t m i -> p m i t"),
                w_raw[d][:].rearrange("p i (m t) -> p m i t", t=PACK)[:, :, :, t0:t1],
            )

        def quantize(codes, scales, src):
            nc.vector.quantize_mx(out=codes.bitcast(FP8X4), scales=scales, in_=src)

        def quantize_w(d, t0, t1):
            ms = slice(t0 * P, t1 * P)
            quantize(w_codes[d][:, ms], w_scales[d][:, ms], w_bf[d][:, t0:t1, :, :].rearrange("p t m i -> p (t m i)"))

        half = J // 2
        t_planes = [ts_got[:], ts_one[:].bitcast(U8)]
        for j0 in (0, half):
            nc.vector.tensor_copy(tw_got[:, j0 : j0 + half], tw_win[:].bitcast(U32).indirect(entries(idx, j0, j0 + half)))
        cast_w(nc.scalar.copy, 1, 0, PACK)
        cast_w(nc.scalar.copy, 2, 0, PACK)
        for h in range(2):
            nc.vector.tensor_copy(
                t_codes[h][:],
                tw_got[:, h * half : (h + 1) * half].bitcast(U16).rearrange("p (n d) -> p d n", d=2),
            )
        quantize_w(1, 0, PACK)
        quantize_w(2, 0, PACK)

        for c in range(NCH):
            js = slice(c * CH, (c + 1) * CH)
            acc = psum.tile([P, PACK, CH], F32, name="acc")
            for t in range(PACK):
                ms = slice(t * P, (t + 1) * P)
                for d in range(2):
                    nc.tensor.matmul_mx(
                        out=acc[:, t, :],
                        lhsT=w_codes[1 + d][:, ms].bitcast(FP8X4),
                        lhsT_scale=w_scales[1 + d][:, ms],
                        rhs=t_codes[c // 4][:, d, (c % 4) * CH : (c % 4 + 1) * CH].bitcast(FP4X4),
                        rhs_scale=t_planes[d][:, js],
                        start=(d == 0),
                        stop=(d == 1),
                    )
            nc.scalar.activation(gate[:, js, :], acc[:].rearrange("p t n -> p n t"), SIGMOID)

        def gather_x(i, j0, j1):
            nc.vector.tensor_tensor(x_got[j0 // half][:, i, j0 % half : j0 % half + j1 - j0], x_pl[i][:].indirect(entries(idx2, j0, j1)), wgt[:, j0:j1], MULT)

        def round_x(j0, j1, i0, i1, copy=nc.scalar.copy):
            copy(
                x_bf[:, j0:j1, i0:i1].rearrange("p (c u) i -> p c i u", u=4),
                x_got[j0 // half][:, i0:i1, j0 % half : j0 % half + j1 - j0].rearrange("p i (c u) -> p c i u", u=4),
            )

        def quantize_x(j0, j1):
            quantize(x_codes[:, j0:j1], x_scales[:, j0:j1], x_bf[:, j0:j1, :].rearrange("p n i -> p (n i)"))

        def gated(c):
            js = slice(c * CH, (c + 1) * CH)
            acc = psum.tile([P, PACK, CH], F32, name="acc")
            for t in range(PACK):
                ms = slice(t * P, (t + 1) * P)
                nc.tensor.matmul_mx(
                    out=acc[:, t, :],
                    lhsT=w_codes[0][:, ms].bitcast(FP8X4),
                    lhsT_scale=w_scales[0][:, ms],
                    rhs=x_codes[:, js].bitcast(FP8X4),
                    rhs_scale=x_scales[:, js],
                    start=True,
                    stop=True,
                )
            nc.vector.tensor_tensor(h_bf[:, js, :], acc[:].rearrange("p t n -> p n t"), gate[:, js, :], MULT)

        out_v = out.rearrange("(a p) j -> p a j", p=P)
        wd_u8 = wd_codes[:].bitcast(U8)
        wd_pl = wd_plane[:].bitcast(U8)

        def quantize_h(j0, j1):
            quantize(h_codes[:, j0:j1], h_scales[:, j0:j1], h_bf[:, j0:j1, :].rearrange("p n i -> p (n i)"))

        def second(j0, j1, who, split=False):
            w = j1 - j0
            per = 4 // len(who)
            y_sb = tile([P, N // P, w], F32, "y_sb%d" % j0)
            for g in range(4 // per):
                yacc = psum.tile([P, per, w], F32, name="yacc")
                for s in range(per):
                    a = per * g + s
                    nc.tensor.matmul_mx(
                        out=yacc[:, s, :],
                        lhsT=wd_u8[:, 2 * P * a : 2 * P * (a + 1)].bitcast(FP4X4),
                        lhsT_scale=wd_pl[:, P * a : P * (a + 1)],
                        rhs=h_codes[:, j0:j1].bitcast(FP8X4),
                        rhs_scale=h_scales[:, j0:j1],
                        start=True,
                        stop=True,
                    )
                sel = slice(per * g, per * (g + 1))
                if who[g] == "V":
                    nc.vector.tensor_tensor(y_sb[:, sel, :], yacc[:], bias[:, sel].unsqueeze(2).to_broadcast([P, per, w]), ADD)
                else:
                    for s in range(per):
                        a = per * g + s
                        nc.scalar.activation(y_sb[:, a, :], yacc[:, s, :], IDENTITY, bias=bias[:, a : a + 1])
                if split:
                    nc.sync.dma_start(out_v[:, sel, j0:j1], y_sb[:, sel, :])
            if not split:
                nc.sync.dma_start(out_v[:, :, j0:j1], y_sb[:])

        gather_x(0, 0, 512)
        gather_x(0, 512, 1024)
        gather_x(1, 0, 512)
        gather_x(1, 512, 1024)
        gather_x(2, 0, 512)
        gather_x(2, 512, 1024)
        cast_w(nc.vector.tensor_copy, 0, 0, 4)
        quantize_w(0, 0, 4)
        gather_x(3, 0, 256)
        round_x(0, 256, 0, 4)
        quantize_x(0, 256)
        gather_x(3, 256, 512)
        round_x(256, 512, 0, 4)
        gather_x(3, 512, 768)
        round_x(512, 768, 0, 4)
        gather_x(3, 768, 1024)
        round_x(768, 1024, 0, 4)
        gated(0)
        gated(1)
        quantize_x(256, 512)
        quantize_x(512, 768)
        gated(2)
        quantize_h(0, 256)
        gated(3)
        gated(4)
        second(0, 256, "SS", True)
        quantize_h(256, 512)
        quantize_x(768, 1024)
        gated(5)
        gated(6)
        second(256, 512, "SS", True)
        quantize_h(512, 768)
        gated(7)
        quantize_h(768, 896)
        quantize_h(896, 1024)
        second(512, 768, "SS", True)
        second(768, 896, "V", True)
        second(896, 1024, "VS", True)
